import numpy as np, ml_dtypes
CORES = [1,3,5,9,11,13]
N = 6
import mx_ref
NC, W = 128, 4
BF = ml_dtypes.bfloat16
def cut(t, i, w=512):
    return t[:, w * i:w * i + w]
def term(a, B):
    return np.stack([mx_ref.matmul(mx_ref.quantize(cut(a, i)), B) for i in range(4)], axis=2).reshape(128, -1)
def setup_inputs(rng):
    def f(*shape):
        return mx_ref.flush((rng.standard_normal(shape, dtype=np.float32) * np.exp2(rng.integers(-2, 3, shape[:-1] + (1,)))).astype(BF))
    return {"a": f(N, 128, 4 * 512), "b": f(N, 128, 4 * NC)}
def setup_inputs_blocks(rng):
    d = setup_inputs(rng)
    for k in ("a", "b"): d[k] = mx_ref.spread(d[k], rng, 2)
    return d
def setup_inputs_wide(rng):
    d = setup_inputs(rng)
    for k in ("a", "b"): d[k] = mx_ref.flush((d[k].astype(np.float32) * np.exp2(rng.integers(-4, 5, (N, 1, 1))).astype(np.float32)).astype(BF))
    return d
def setup_inputs_lossless(rng):
    a = np.zeros((N, 128, 4 * 128, 4), np.float32)
    for r in range(N):
        k = rng.integers(0, 512, size=4 * 128)
        a[r, k // 4, np.arange(4 * 128), k % 4] = 1.0
    size = np.repeat(2.0 ** rng.integers(-4, 5, size=(1, 1, (4 * NC) // 4)), 4, axis=2)
    b = rng.integers(-1, 2, size=(N, 128, 4 * NC)) * size
    return {"a": a.reshape(N, 128, 4 * 512).astype(BF), "b": b.astype(np.float32).astype(BF)}
def reference(a, b):
    T = [term(a[r], mx_ref.quantize(b[r])) for r in range(N)]
    y = np.zeros((N, 128, 4 * NC), np.float32)
    for c in range(N):
        y[c] = mx_ref.total([T[(c - k) % N] for k in range(W)])
    return {"y": y}

@@ -1,0 +1,198 @@
+from concourse.mybir import dt, AluOpType, ActivationFunctionType
+
+SIM = 16
+W = 4
+NCOL = 128
+TW = W * NCOL
+BANK = 512
+CODES = "float8_e4m3fn_x4"
+CUT = 3
+
+SCRATCH = {
+    "ta": ("sbuf", [128, W * TW], "bfloat16"),
+    "tb": ("sbuf", [128, TW], "bfloat16"),
+    "sel": ("sbuf", [128, TW + W], "bfloat16"),
+    "t": ("sbuf", [128, TW], "bfloat16"),
+    "t2": ("sbuf", [128, TW], "bfloat16"),
+    "yo": ("sbuf", [128, TW], "float32"),
+    "qs": ("sbuf", [128, TW], CODES), "ps": ("sbuf", [128, TW], "uint8"),
+    "qa": ("sbuf", [128, TW], CODES), "pa": ("sbuf", [128, TW], "uint8"),
+    "qb": ("sbuf", [128, NCOL], CODES), "pb": ("sbuf", [128, NCOL], "uint8"),
+    "qt": ("sbuf", [128, NCOL], CODES), "pt": ("sbuf", [128, NCOL], "uint8"),
+    "qu": ("sbuf", [128, NCOL], CODES), "pu": ("sbuf", [128, NCOL], "uint8"),
+    "xa": ("sbuf", [128, NCOL], CODES), "za": ("sbuf", [128, NCOL], "uint8"),
+    "xb": ("sbuf", [128, NCOL], CODES), "zb": ("sbuf", [128, NCOL], "uint8"),
+    "acc": ("psum", [128, 2 * W * BANK], "float32"),
+}
+SEMAPHORES = (["ld_b", "ld_0", "ld_1", "ones", "sel", "qs", "qb", "sent", "stored", "qt", "qu",
+               "xa_c", "xa_s", "xb_c", "xb_s"]
+              + ["qa%d" % i for i in range(W)] + ["m%d" % i for i in range(W)]
+              + ["u%d" % i for i in range(W)] + ["y%d" % i for i in range(W)]
+              + ["mv", "ms", "uv", "us", "yv", "ys"])
+
+
+def roles(T, topo):
+    out = []
+    n = len(T.cores) // 2
+    for h in range(2):
+        tri = T.cores[n * h:n * h + n]
+        far = T.cores[n * (1 - h)]
+        free = [c for c in range(SIM) if T.rank_of(c) is None and topo.chip(c) == topo.chip(tri[0])
+                and topo.may_write(c, far)]
+        out.append({"lo": tri[0], "mid": tri[1], "hi": tri[2],
+                    "s": [c for c in free if topo.die(c) == topo.die(tri[2])][-1],
+                    "f": [c for c in free if topo.die(c) != topo.die(tri[2])][0]})
+    return out
+
+
+def rank_program(g, core, T, topo):
+    both = roles(T, topo)
+    home = [r for r in both if topo.chip(r["lo"]) == topo.chip(core)][0]
+    far = [r for r in both if r is not home][0]
+    role = ([k for k in home if home[k] == core] or [None])[0]
+    if role is None:
+        return
+    sem = T.sem
+    sent = [0]
+
+    def send(dst, src, land, codes):
+        m = topo.mask(core, dst)
+        eng = [e for e in range(m.bit_length()) if (m >> e) & 1]
+        if topo.chip(core) == topo.chip(dst):
+            eng = eng[::2]
+        m = sum(1 << e for e in eng)
+        rid, pid, _ = topo.addr(dst)
+        if codes:
+            o, i, s = T["x" + land][:].bitcast(dt.uint8), T[src][:].bitcast(dt.uint8), sem["x" + land + "_c"]
+        else:
+            o, i, s = T["z" + land][:], T[src][:], sem["x" + land + "_s"]
+        g.remote_dma(o, i, s, sem.sent, pid, rid, m)
+        sent[0] += len(eng)
+
+    full = 8
+
+    def wait_in(q, land):
+        q.wait_ge(sem["x" + land + "_c"], full)
+        q.wait_ge(sem["x" + land + "_s"], full)
+
+    if role == "f":
+        g.wait_ge(sem.xb_c, full)
+        send(far["lo"], "xb", "b", True)
+        g.wait_ge(sem.xb_s, full)
+        send(far["lo"], "zb", "b", False)
+        g.wait_ge(sem.sent, sent[0])
+        return
+
+    v, pe, act = g.vector, g.tensor, g.scalar
+
+    def w(i):
+        return slice(NCOL * i, NCOL * i + NCOL)
+
+    def bank(k, i):
+        o = BANK * (W * k + i)
+        return T.acc[:, o:o + NCOL]
+
+    if role != "s":
+        act.dma_start(T.tb[:], T.b[:]).then_inc(sem.ld_b, 16)
+        g.sync.dma_start(T.ta[:, :TW * CUT], T.a[:, :TW * CUT]).then_inc(sem.ld_0, 16)
+        g.sync.dma_start(T.ta[:, TW * CUT:], T.a[:, TW * CUT:]).then_inc(sem.ld_1, 16)
+
+    v.memset(T.sel[:], 1.0).then_inc(sem.ones, 1)
+    g.wait_ge(sem.ones, 1)
+    g.affine_select(T.sel[:], T.sel[:], [[-1, TW + W]], AluOpType.is_equal, 0.0, W - 1, W).then_inc(sem.sel, 1)
+    v.wait_ge(sem.sel, 1)
+    for i in range(W):
+        v.quantize_mx(T.qs[:, w(i)], T.ps[:, w(i)], T.sel[:, W - 1 - i:W - 1 - i + TW]).then_inc(sem.qs, 1)
+
+    def products(k, last):
+        for i in range(W):
+            pe.matmul_mx(bank(k, i), T.qa[:, w(i)], T.pa[:, w(i)], T.qb[:], T.pb[:], True, last)
+
+    def add(k, land, first, last, done=None):
+        for i in range(W):
+            c = pe.matmul_mx(bank(k, i), T.qs[:, w(i)], T.ps[:, w(i)], T["x" + land][:], T["z" + land][:], first, last)
+            if done:
+                c.then_inc(sem["%s%d" % (done, i)], 1)
+
+    def out_of_psum(k, ev, tile, on_act):
+        for i in range(W):
+            o = T[tile][:, i:TW:W]
+            q = act if i in on_act else v
+            q.wait_ge(sem["%s%d" % (ev, i)], 1)
+            if i in on_act:
+                act.activation(o, bank(k, i), ActivationFunctionType.Copy).then_inc(sem[ev + "s"], 1)
+            else:
+                v.tensor_copy(o, bank(k, i)).then_inc(sem[ev + "v"], 1)
+
+    def quantise(ev, tile, q, p, done, on_act):
+        v.wait_ge(sem[ev + "s"], len(on_act))
+        v.wait_ge(sem[ev + "v"], W - len(on_act))
+        v.quantize_mx(T[q][:], T[p][:], T[tile][:]).then_inc(sem[done], 1)
+
+    alt = [0, 2]
+
+    if role == "s":
+        pe.wait_ge(sem.qs, W)
+        wait_in(pe, "a")
+        add(0, "a", True, False)
+        wait_in(pe, "b")
+        add(0, "b", False, True, "m")
+        out_of_psum(0, "m", "t", alt)
+        quantise("m", "t", "qt", "pt", "qt", alt)
+        g.wait_ge(sem.xb_c, full)
+        send(far["hi"], "xb", "b", True)
+        g.wait_ge(sem.xb_s, full)
+        send(far["hi"], "zb", "b", False)
+        g.wait_ge(sem.qt, 1)
+        send(far["mid"], "qt", "b", True)
+        send(far["mid"], "pt", "b", False)
+        g.wait_ge(sem.sent, sent[0])
+        return
+
+    v.wait_ge(sem.ld_b, 16)
+    v.quantize_mx(T.qb[:], T.pb[:], T.tb[:]).then_inc(sem.qb, 1)
+    for i in range(W):
+        if i in (0, CUT):
+            v.wait_ge(sem["ld_%d" % (i // CUT)], 16)
+        v.quantize_mx(T.qa[:, w(i)], T.pa[:, w(i)], T.ta[:, TW * i:TW * i + TW]).then_inc(sem["qa%d" % i], 1)
+    pe.wait_ge(sem.qb, 1)
+    for i in range(W):
+        pe.wait_ge(sem["qa%d" % i], 1)
+        pe.matmul_mx(bank(0, i), T.qa[:, w(i)], T.pa[:, w(i)], T.qb[:], T.pb[:], True, True).then_inc(sem["m%d" % i], 1)
+    early = list(range(CUT))
+    out_of_psum(0, "m", "t", early)
+    quantise("m", "t", "qt", "pt", "qt", early)
+
+    g.wait_ge(sem.qt, 1)
+    for dst, land in {"lo": [("mid", "a")], "mid": [("s", "a")], "hi": [("s", "b"), ("f", "b")]}[role]:
+        send(home[dst], "qt", land, True)
+        send(home[dst], "pt", land, False)
+
+    yk = 1
+    products(1, False)
+    pe.wait_ge(sem.qs, W)
+    if role == "mid":
+        wait_in(pe, "a")
+        add(1, "a", False, True, "u")
+        out_of_psum(1, "u", "t2", alt)
+        quantise("u", "t2", "qu", "pu", "qu", alt)
+        g.wait_ge(sem.qu, 1)
+        for dst in (far["lo"], home["hi"]):
+            send(dst, "qu", "a", True)
+            send(dst, "pu", "a", False)
+        yk = 0
+        pe.wait_ge(sem.qt, 1)
+        products(0, False)
+        order = ("a", "b")
+    else:
+        order = ("a", "b") if role == "lo" else ("b", "a")
+
+    for n, land in enumerate(order):
+        wait_in(pe, land)
+        add(yk, land, False, n == 1, "y" if n == 1 else None)
+    out_of_psum(yk, "y", "yo", alt)
+    g.sync.wait_ge(sem.ys, len(alt))
+    g.sync.wait_ge(sem.yv, W - len(alt))
+    g.sync.dma_start(T.y[:], T.yo[:]).then_inc(sem.stored, 16)
+    g.sync.wait_ge(sem.stored, 16)
+    g.wait_ge(sem.sent, sent[0])

@@ -1,3 +1,4 @@
+from concourse.bass import DstId, RemoteDMATransfer
 from concourse.mybir import dt, AluOpType, ActivationFunctionType
 
 SIM = 16
@@ -7,6 +8,7 @@ TW = W * NCOL
 BANK = 512
 CODES = "float8_e4m3fn_x4"
 CUT = 3
+FULL = 8
 
 SCRATCH = {
     "ta": ("sbuf", [128, W * TW], "bfloat16"),
@@ -26,9 +28,8 @@ SCRATCH = {
 }
 SEMAPHORES = (["ld_b", "ld_0", "ld_1", "ones", "sel", "qs", "qb", "sent", "stored", "qt", "qu",
                "xa_c", "xa_s", "xb_c", "xb_s"]
-              + ["qa%d" % i for i in range(W)] + ["m%d" % i for i in range(W)]
-              + ["u%d" % i for i in range(W)] + ["y%d" % i for i in range(W)]
-              + ["mv", "ms", "uv", "us", "yv", "ys"])
+              + ["%s%d" % (k, i) for k in ("qa", "m", "u", "y", "e") for i in range(W)]
+              + ["mv", "ms", "uv", "us"])
 
 
 def roles(T, topo):
@@ -55,31 +56,37 @@ def rank_program(g, core, T, topo):
     sem = T.sem
     sent = [0]
 
-    def send(dst, src, land, codes):
-        m = topo.mask(core, dst)
-        eng = [e for e in range(m.bit_length()) if (m >> e) & 1]
-        if topo.chip(core) == topo.chip(dst):
-            eng = eng[::2]
-        m = sum(1 << e for e in eng)
-        rid, pid, _ = topo.addr(dst)
-        if codes:
-            o, i, s = T["x" + land][:].bitcast(dt.uint8), T[src][:].bitcast(dt.uint8), sem["x" + land + "_c"]
+    def send(dsts, codes, src, land):
+        tr, used = [], 0
+        for dst in dsts:
+            m = topo.mask(core, dst)
+            eng = [e for e in range(m.bit_length()) if (m >> e) & 1 and not (used >> e) & 1]
+            eng = eng[::max(1, len(eng) // FULL)][:FULL]
+            m = sum(1 << e for e in eng)
+            used |= m
+            rid, pid, _ = topo.addr(dst)
+            if codes:
+                o, i, s = T["x" + land][:].bitcast(dt.uint8), T[src][:].bitcast(dt.uint8), sem["x" + land + "_c"]
+            else:
+                o, i, s = T["z" + land][:], T[src][:], sem["x" + land + "_s"]
+            tr.append((rid, pid, m, o, i, s))
+            sent[0] += len(eng)
+        if len(tr) == 1:
+            rid, pid, m, o, i, s = tr[0]
+            g.remote_dma(o, i, s, sem.sent, pid, rid, m)
         else:
-            o, i, s = T["z" + land][:], T[src][:], sem["x" + land + "_s"]
-        g.remote_dma(o, i, s, sem.sent, pid, rid, m)
-        sent[0] += len(eng)
-
-    full = 8
+            g.remote_dma_fused([RemoteDMATransfer(dst_ids=[DstId(rid=rid, pnc=pid)], dma_engine_mask=m, remote_sem=s,
+                                                  src=i, dst=o) for rid, pid, m, o, i, s in tr], local_sem=sem.sent)
 
     def wait_in(q, land):
-        q.wait_ge(sem["x" + land + "_c"], full)
-        q.wait_ge(sem["x" + land + "_s"], full)
+        q.wait_ge(sem["x" + land + "_c"], FULL)
+        q.wait_ge(sem["x" + land + "_s"], FULL)
 
     if role == "f":
-        g.wait_ge(sem.xb_c, full)
-        send(far["lo"], "xb", "b", True)
-        g.wait_ge(sem.xb_s, full)
-        send(far["lo"], "zb", "b", False)
+        g.wait_ge(sem.xb_c, FULL)
+        send([far["lo"]], True, "xb", "b")
+        g.wait_ge(sem.xb_s, FULL)
+        send([far["lo"]], False, "zb", "b")
         g.wait_ge(sem.sent, sent[0])
         return
 
@@ -88,9 +95,9 @@ def rank_program(g, core, T, topo):
     def w(i):
         return slice(NCOL * i, NCOL * i + NCOL)
 
-    def bank(k, i):
+    def bank(k, i, part=slice(0, NCOL)):
         o = BANK * (W * k + i)
-        return T.acc[:, o:o + NCOL]
+        return T.acc[:, o + part.start:o + part.stop]
 
     if role != "s":
         act.dma_start(T.tb[:], T.b[:]).then_inc(sem.ld_b, 16)
@@ -100,52 +107,49 @@ def rank_program(g, core, T, topo):
     v.memset(T.sel[:], 1.0).then_inc(sem.ones, 1)
     g.wait_ge(sem.ones, 1)
     g.affine_select(T.sel[:], T.sel[:], [[-1, TW + W]], AluOpType.is_equal, 0.0, W - 1, W).then_inc(sem.sel, 1)
-    v.wait_ge(sem.sel, 1)
-    for i in range(W):
-        v.quantize_mx(T.qs[:, w(i)], T.ps[:, w(i)], T.sel[:, W - 1 - i:W - 1 - i + TW]).then_inc(sem.qs, 1)
 
-    def products(k, last):
+    def selectors():
+        v.wait_ge(sem.sel, 1)
         for i in range(W):
-            pe.matmul_mx(bank(k, i), T.qa[:, w(i)], T.pa[:, w(i)], T.qb[:], T.pb[:], True, last)
+            v.quantize_mx(T.qs[:, w(i)], T.ps[:, w(i)], T.sel[:, W - 1 - i:W - 1 - i + TW]).then_inc(sem.qs, 1)
 
-    def add(k, land, first, last, done=None):
+    def add(k, codes, plane, first, last, done=None):
         for i in range(W):
-            c = pe.matmul_mx(bank(k, i), T.qs[:, w(i)], T.ps[:, w(i)], T["x" + land][:], T["z" + land][:], first, last)
+            c = pe.matmul_mx(bank(k, i), T.qs[:, w(i)], T.ps[:, w(i)], T[codes][:], T[plane][:], first, last)
             if done:
                 c.then_inc(sem["%s%d" % (done, i)], 1)
 
-    def out_of_psum(k, ev, tile, on_act):
-        for i in range(W):
-            o = T[tile][:, i:TW:W]
-            q = act if i in on_act else v
-            q.wait_ge(sem["%s%d" % (ev, i)], 1)
-            if i in on_act:
-                act.activation(o, bank(k, i), ActivationFunctionType.Copy).then_inc(sem[ev + "s"], 1)
-            else:
-                v.tensor_copy(o, bank(k, i)).then_inc(sem[ev + "v"], 1)
-
-    def quantise(ev, tile, q, p, done, on_act):
-        v.wait_ge(sem[ev + "s"], len(on_act))
-        v.wait_ge(sem[ev + "v"], W - len(on_act))
-        v.quantize_mx(T[q][:], T[p][:], T[tile][:]).then_inc(sem[done], 1)
+    def copy(on_act, out, in_):
+        if on_act:
+            return act.activation(out, in_, ActivationFunctionType.Copy)
+        return v.tensor_copy(out, in_)
 
     alt = [0, 2]
 
+    def requantise(k, ev, tile, q, p, done):
+        for i in range(W):
+            a = i in alt
+            (act if a else v).wait_ge(sem["%s%d" % (ev, i)], 1)
+            copy(a, T[tile][:, i:TW:W], bank(k, i)).then_inc(sem[ev + ("s" if a else "v")], 1)
+        v.wait_ge(sem[ev + "s"], len(alt))
+        v.wait_ge(sem[ev + "v"], W - len(alt))
+        v.quantize_mx(T[q][:], T[p][:], T[tile][:]).then_inc(sem[done], 1)
+
     if role == "s":
+        selectors()
         pe.wait_ge(sem.qs, W)
         wait_in(pe, "a")
-        add(0, "a", True, False)
+        add(0, "xa", "za", True, False)
         wait_in(pe, "b")
-        add(0, "b", False, True, "m")
-        out_of_psum(0, "m", "t", alt)
-        quantise("m", "t", "qt", "pt", "qt", alt)
-        g.wait_ge(sem.xb_c, full)
-        send(far["hi"], "xb", "b", True)
-        g.wait_ge(sem.xb_s, full)
-        send(far["hi"], "zb", "b", False)
+        add(0, "xb", "zb", False, True, "m")
+        requantise(0, "m", "t", "qt", "pt", "qt")
+        g.wait_ge(sem.xb_c, FULL)
+        send([far["hi"]], True, "xb", "b")
+        g.wait_ge(sem.xb_s, FULL)
+        send([far["hi"]], False, "zb", "b")
         g.wait_ge(sem.qt, 1)
-        send(far["mid"], "qt", "b", True)
-        send(far["mid"], "pt", "b", False)
+        send([far["mid"]], True, "qt", "b")
+        send([far["mid"]], False, "pt", "b")
         g.wait_ge(sem.sent, sent[0])
         return
 
@@ -159,40 +163,51 @@ def rank_program(g, core, T, topo):
     for i in range(W):
         pe.wait_ge(sem["qa%d" % i], 1)
         pe.matmul_mx(bank(0, i), T.qa[:, w(i)], T.pa[:, w(i)], T.qb[:], T.pb[:], True, True).then_inc(sem["m%d" % i], 1)
-    early = list(range(CUT))
-    out_of_psum(0, "m", "t", early)
-    quantise("m", "t", "qt", "pt", "qt", early)
+    half = NCOL // 2
+    for i in range(W):
+        a = i < CUT
+        (act if a else v).wait_ge(sem["m%d" % i], 1)
+        for h in range(2):
+            copy(a, T.t[:, 4 * (i // 2) + 2 * h + i % 2:TW:8], bank(0, i, slice(half * h, half * h + half))).then_inc(
+                sem["ms" if a else "mv"], 1)
+    v.wait_ge(sem.ms, 2 * CUT)
+    v.wait_ge(sem.mv, 2 * (W - CUT))
+    v.quantize_mx(T.qt[:], T.pt[:], T.t[:]).then_inc(sem.qt, 1)
+    selectors()
 
+    dsts, land = {"lo": (["mid"], "a"), "mid": (["s"], "a"), "hi": (["s", "f"], "b")}[role]
     g.wait_ge(sem.qt, 1)
-    for dst, land in {"lo": [("mid", "a")], "mid": [("s", "a")], "hi": [("s", "b"), ("f", "b")]}[role]:
-        send(home[dst], "qt", land, True)
-        send(home[dst], "pt", land, False)
+    send([home[d] for d in dsts], True, "qt", land)
+    send([home[d] for d in dsts], False, "pt", land)
 
-    yk = 1
-    products(1, False)
+    pe.wait_ge(sem.qt, 1)
     pe.wait_ge(sem.qs, W)
+    yk = 1
+    add(1, "qt", "pt", True, False)
+    order = ("b", "a")
     if role == "mid":
         wait_in(pe, "a")
-        add(1, "a", False, True, "u")
-        out_of_psum(1, "u", "t2", alt)
-        quantise("u", "t2", "qu", "pu", "qu", alt)
+        add(1, "xa", "za", False, True, "u")
+        requantise(1, "u", "t2", "qu", "pu", "qu")
         g.wait_ge(sem.qu, 1)
-        for dst in (far["lo"], home["hi"]):
-            send(dst, "qu", "a", True)
-            send(dst, "pu", "a", False)
+        send([far["lo"], home["hi"]], True, "qu", "a")
+        send([far["lo"], home["hi"]], False, "pu", "a")
         yk = 0
-        pe.wait_ge(sem.qt, 1)
-        products(0, False)
+        add(0, "qt", "pt", True, False)
         order = ("a", "b")
-    else:
-        order = ("a", "b") if role == "lo" else ("b", "a")
 
-    for n, land in enumerate(order):
-        wait_in(pe, land)
-        add(yk, land, False, n == 1, "y" if n == 1 else None)
-    out_of_psum(yk, "y", "yo", alt)
-    g.sync.wait_ge(sem.ys, len(alt))
-    g.sync.wait_ge(sem.yv, W - len(alt))
-    g.sync.dma_start(T.y[:], T.yo[:]).then_inc(sem.stored, 16)
-    g.sync.wait_ge(sem.stored, 16)
+    for n, x in enumerate(order):
+        wait_in(pe, x)
+        add(yk, "x" + x, "z" + x, False, n == 1, "y" if n == 1 else None)
+    for i in range(W):
+        a = i in alt
+        (act if a else v).wait_ge(sem["y%d" % i], 1)
+        o = (TW // 2) * (i // 2)
+        copy(a, T.yo[:, o + i % 2:o + TW // 2:2], bank(yk, i)).then_inc(sem["e%d" % i], 1)
+    for h in range(2):
+        g.sync.wait_ge(sem["e%d" % (2 * h)], 1)
+        g.sync.wait_ge(sem["e%d" % (2 * h + 1)], 1)
+        cols = slice(TW // 2 * h, TW // 2 * h + TW // 2)
+        g.sync.dma_start(T.y[:, cols], T.yo[:, cols]).then_inc(sem.stored, 16)
+    g.sync.wait_ge(sem.stored, 32)
     g.wait_ge(sem.sent, sent[0])

@@ -4,32 +4,37 @@ from concourse.mybir import dt, AluOpType, ActivationFunctionType
 SIM = 16
 W = 4
 NCOL = 128
+H = NCOL // 2
 TW = W * NCOL
+HW = TW // 2
 BANK = 512
 CODES = "float8_e4m3fn_x4"
-CUT = 3
-FULL = 8
+WIDE = 8
 
 SCRATCH = {
     "ta": ("sbuf", [128, W * TW], "bfloat16"),
     "tb": ("sbuf", [128, TW], "bfloat16"),
     "sel": ("sbuf", [128, TW + W], "bfloat16"),
-    "t": ("sbuf", [128, TW], "bfloat16"),
-    "t2": ("sbuf", [128, TW], "bfloat16"),
+    "t": ("sbuf", [128, 3 * HW], "bfloat16"),
+    "tu": ("sbuf", [128, TW], "bfloat16"),
     "yo": ("sbuf", [128, TW], "float32"),
-    "qs": ("sbuf", [128, TW], CODES), "ps": ("sbuf", [128, TW], "uint8"),
-    "qa": ("sbuf", [128, TW], CODES), "pa": ("sbuf", [128, TW], "uint8"),
-    "qb": ("sbuf", [128, NCOL], CODES), "pb": ("sbuf", [128, NCOL], "uint8"),
-    "qt": ("sbuf", [128, NCOL], CODES), "pt": ("sbuf", [128, NCOL], "uint8"),
-    "qu": ("sbuf", [128, NCOL], CODES), "pu": ("sbuf", [128, NCOL], "uint8"),
-    "xa": ("sbuf", [128, NCOL], CODES), "za": ("sbuf", [128, NCOL], "uint8"),
-    "xb": ("sbuf", [128, NCOL], CODES), "zb": ("sbuf", [128, NCOL], "uint8"),
     "acc": ("psum", [128, 2 * W * BANK], "float32"),
 }
-SEMAPHORES = (["ld_b", "ld_0", "ld_1", "ones", "sel", "qs", "qb", "sent", "stored", "qt", "qu",
-               "xa_c", "xa_s", "xb_c", "xb_s"]
-              + ["%s%d" % (k, i) for k in ("qa", "m", "u", "y", "e") for i in range(W)]
-              + ["mv", "ms", "uv", "us"])
+for _k, _n in {"s": TW,
+               "a": TW, "b": NCOL,
+               "q": NCOL,
+               "t": NCOL,
+               "u": NCOL,
+               "x": NCOL,
+               "y": NCOL,
+               }.items():
+    SCRATCH["c" + _k] = ("sbuf", [128, _n], CODES)
+    SCRATCH["p" + _k] = ("sbuf", [128, _n], "uint8")
+
+SEMAPHORES = (["ld_b", "ld_0", "ld_1", "ones", "sel", "zero", "qs", "qb", "q1", "qt", "qu", "sent", "stored"]
+              + ["%s%s%s" % (b, k, p) for b in "xy" for k in "cp" for p in "12w"]
+              + ["%s%d" % (k, i) for k in ("qa", "m", "k", "u", "v", "y", "e") for i in range(W)])
+PART = {"1": slice(0, H), "2": slice(H, NCOL), "w": slice(0, NCOL)}
 
 
 def roles(T, topo):
@@ -56,37 +61,45 @@ def rank_program(g, core, T, topo):
     sem = T.sem
     sent = [0]
 
-    def send(dsts, codes, src, land):
-        tr, used = [], 0
-        for dst in dsts:
-            m = topo.mask(core, dst)
-            eng = [e for e in range(m.bit_length()) if (m >> e) & 1 and not (used >> e) & 1]
-            eng = eng[::max(1, len(eng) // FULL)][:FULL]
-            m = sum(1 << e for e in eng)
-            used |= m
+    def engines(m):
+        return [e for e in range(m.bit_length()) if (m >> e) & 1]
+
+    def send(kind, part, src, at, *moves):
+        n = PART[part].stop - PART[part].start
+        tr = []
+        for dst, buf, eng in moves:
             rid, pid, _ = topo.addr(dst)
-            if codes:
-                o, i, s = T["x" + land][:].bitcast(dt.uint8), T[src][:].bitcast(dt.uint8), sem["x" + land + "_c"]
-            else:
-                o, i, s = T["z" + land][:], T[src][:], sem["x" + land + "_s"]
-            tr.append((rid, pid, m, o, i, s))
+            o, i = T[kind + buf][:, PART[part]], T[kind + src][:, at:at + n]
+            if kind == "c":
+                o, i = o.bitcast(dt.uint8), i.bitcast(dt.uint8)
+            tr.append((o, i, sem[buf + kind + part], pid, rid, sum(1 << e for e in eng)))
             sent[0] += len(eng)
         if len(tr) == 1:
-            rid, pid, m, o, i, s = tr[0]
+            o, i, s, pid, rid, m = tr[0]
             g.remote_dma(o, i, s, sem.sent, pid, rid, m)
         else:
             g.remote_dma_fused([RemoteDMATransfer(dst_ids=[DstId(rid=rid, pnc=pid)], dma_engine_mask=m, remote_sem=s,
-                                                  src=i, dst=o) for rid, pid, m, o, i, s in tr], local_sem=sem.sent)
+                                                  src=i, dst=o) for o, i, s, pid, rid, m in tr], local_sem=sem.sent)
 
-    def wait_in(q, land):
-        q.wait_ge(sem["x" + land + "_c"], FULL)
-        q.wait_ge(sem["x" + land + "_s"], FULL)
+    def wait_in(q, buf, *arrivals):
+        for a in arrivals:
+            q.wait_ge(sem[buf + a], WIDE)
+
+    here = engines(topo.mask(core, home["lo" if role != "lo" else "hi"]))
+    even, odd = here[0::2], here[1::2]
+    if role in ("mid", "s", "f"):
+        out = engines(topo.mask(core, far["lo"]))
+        stay = [e for e in here if e not in out]
+
+    def relay(dst):
+        for part, at in (("1", 0), ("2", H)):
+            wait_in(g, "y", "c" + part)
+            send("c", part, "y", at, (dst, "y", out))
+        wait_in(g, "y", "p1", "p2")
+        send("p", "w", "y", 0, (dst, "y", out))
 
     if role == "f":
-        g.wait_ge(sem.xb_c, FULL)
-        send([far["lo"]], True, "xb", "b")
-        g.wait_ge(sem.xb_s, FULL)
-        send([far["lo"]], False, "zb", "b")
+        relay(far["lo"])
         g.wait_ge(sem.sent, sent[0])
         return
 
@@ -95,14 +108,15 @@ def rank_program(g, core, T, topo):
     def w(i):
         return slice(NCOL * i, NCOL * i + NCOL)
 
-    def bank(k, i, part=slice(0, NCOL)):
-        o = BANK * (W * k + i)
-        return T.acc[:, o + part.start:o + part.stop]
+    def bank(k, i, lo=0, n=NCOL):
+        o = BANK * (W * k + i) + lo
+        return T.acc[:, o:o + n]
 
     if role != "s":
         act.dma_start(T.tb[:], T.b[:]).then_inc(sem.ld_b, 16)
-        g.sync.dma_start(T.ta[:, :TW * CUT], T.a[:, :TW * CUT]).then_inc(sem.ld_0, 16)
-        g.sync.dma_start(T.ta[:, TW * CUT:], T.a[:, TW * CUT:]).then_inc(sem.ld_1, 16)
+        for k in range(2):
+            cols = slice(2 * TW * k, 2 * TW * k + 2 * TW)
+            g.sync.dma_start(T.ta[:, cols], T.a[:, cols]).then_inc(sem["ld_%d" % k], 16)
 
     v.memset(T.sel[:], 1.0).then_inc(sem.ones, 1)
     g.wait_ge(sem.ones, 1)
@@ -111,103 +125,108 @@ def rank_program(g, core, T, topo):
     def selectors():
         v.wait_ge(sem.sel, 1)
         for i in range(W):
-            v.quantize_mx(T.qs[:, w(i)], T.ps[:, w(i)], T.sel[:, W - 1 - i:W - 1 - i + TW]).then_inc(sem.qs, 1)
+            v.quantize_mx(T.cs[:, w(i)], T.ps[:, w(i)], T.sel[:, W - 1 - i:W - 1 - i + TW]).then_inc(sem.qs, 1)
 
-    def add(k, codes, plane, first, last, done=None):
+    def add(k, buf, first, last, done=None):
         for i in range(W):
-            c = pe.matmul_mx(bank(k, i), T.qs[:, w(i)], T.ps[:, w(i)], T[codes][:], T[plane][:], first, last)
+            c = pe.matmul_mx(bank(k, i), T.cs[:, w(i)], T.ps[:, w(i)], T["c" + buf][:, :NCOL], T["p" + buf][:, :NCOL], first, last)
             if done:
                 c.then_inc(sem["%s%d" % (done, i)], 1)
 
-    def copy(on_act, out, in_):
+    def copy(on_act, out_, in_):
         if on_act:
-            return act.activation(out, in_, ActivationFunctionType.Copy)
-        return v.tensor_copy(out, in_)
+            return act.activation(out_, in_, ActivationFunctionType.Copy)
+        return v.tensor_copy(out_, in_)
 
-    alt = [0, 2]
-
-    def requantise(k, ev, tile, q, p, done):
+    def requantise(k):
         for i in range(W):
-            a = i in alt
-            (act if a else v).wait_ge(sem["%s%d" % (ev, i)], 1)
-            copy(a, T[tile][:, i:TW:W], bank(k, i)).then_inc(sem[ev + ("s" if a else "v")], 1)
-        v.wait_ge(sem[ev + "s"], len(alt))
-        v.wait_ge(sem[ev + "v"], W - len(alt))
-        v.quantize_mx(T[q][:], T[p][:], T[tile][:]).then_inc(sem[done], 1)
+            a = i % 2 == 0
+            (act if a else v).wait_ge(sem["u%d" % i], 1)
+            copy(a, T.tu[:, i:TW:W], bank(k, i)).then_inc(sem["v%d" % i], 1)
+        for i in range(W):
+            v.wait_ge(sem["v%d" % i], 1)
+        v.quantize_mx(T.cu[:], T.pu[:], T.tu[:]).then_inc(sem.qu, 1)
+
+    halves = ("c1", "p1", "c2", "p2")
 
     if role == "s":
         selectors()
         pe.wait_ge(sem.qs, W)
-        wait_in(pe, "a")
-        add(0, "xa", "za", True, False)
-        wait_in(pe, "b")
-        add(0, "xb", "zb", False, True, "m")
-        requantise(0, "m", "t", "qt", "pt", "qt")
-        g.wait_ge(sem.xb_c, FULL)
-        send([far["hi"]], True, "xb", "b")
-        g.wait_ge(sem.xb_s, FULL)
-        send([far["hi"]], False, "zb", "b")
-        g.wait_ge(sem.qt, 1)
-        send([far["mid"]], True, "qt", "b")
-        send([far["mid"]], False, "pt", "b")
+        wait_in(pe, "x", *halves)
+        add(0, "x", True, False)
+        wait_in(pe, "y", *halves)
+        add(0, "y", False, True, "u")
+        requantise(0)
+        relay(far["hi"])
+        g.wait_ge(sem.qu, 1)
+        for kind in "cp":
+            send(kind, "w", "u", 0, (far["mid"], "y", out))
         g.wait_ge(sem.sent, sent[0])
         return
 
+    v.memset(T.t[:, :HW], 0.0).then_inc(sem.zero, 1)
     v.wait_ge(sem.ld_b, 16)
-    v.quantize_mx(T.qb[:], T.pb[:], T.tb[:]).then_inc(sem.qb, 1)
-    for i in range(W):
-        if i in (0, CUT):
-            v.wait_ge(sem["ld_%d" % (i // CUT)], 16)
-        v.quantize_mx(T.qa[:, w(i)], T.pa[:, w(i)], T.ta[:, TW * i:TW * i + TW]).then_inc(sem["qa%d" % i], 1)
+    v.quantize_mx(T.cb[:], T.pb[:], T.tb[:]).then_inc(sem.qb, 1)
     pe.wait_ge(sem.qb, 1)
-    for i in range(W):
-        pe.wait_ge(sem["qa%d" % i], 1)
-        pe.matmul_mx(bank(0, i), T.qa[:, w(i)], T.pa[:, w(i)], T.qb[:], T.pb[:], True, True).then_inc(sem["m%d" % i], 1)
-    half = NCOL // 2
-    for i in range(W):
-        a = i < CUT
-        (act if a else v).wait_ge(sem["m%d" % i], 1)
-        for h in range(2):
-            copy(a, T.t[:, 4 * (i // 2) + 2 * h + i % 2:TW:8], bank(0, i, slice(half * h, half * h + half))).then_inc(
-                sem["ms" if a else "mv"], 1)
-    v.wait_ge(sem.ms, 2 * CUT)
-    v.wait_ge(sem.mv, 2 * (W - CUT))
-    v.quantize_mx(T.qt[:], T.pt[:], T.t[:]).then_inc(sem.qt, 1)
+    for k in range(2):
+        v.wait_ge(sem["ld_%d" % k], 16)
+        for i in (2 * k, 2 * k + 1):
+            v.quantize_mx(T.ca[:, w(i)], T.pa[:, w(i)], T.ta[:, TW * i:TW * i + TW]).then_inc(sem["qa%d" % i], 1)
+            pe.wait_ge(sem["qa%d" % i], 1)
+            pe.matmul_mx(bank(0, i), T.ca[:, w(i)], T.pa[:, w(i)], T.cb[:], T.pb[:], True, True).then_inc(sem["m%d" % i], 1)
+        for b in range(2):
+            i = 2 * k + b
+            (v if b else act).wait_ge(sem["m%d" % i], 1)
+            for h in range(2):
+                o = HW * (1 + k)
+                copy(b == 0, T.t[:, o + 2 * h + b:o + HW:W], bank(0, i, H * h, H)).then_inc(sem["k%d" % i], 1)
+        v.wait_ge(sem["k%d" % (2 * k)], 2)
+        v.wait_ge(sem["k%d" % (2 * k + 1)], 2)
+        if k == 0:
+            v.wait_ge(sem.zero, 1)
+            v.quantize_mx(T.cq[:], T.pq[:], T.t[:, :TW]).then_inc(sem.q1, 1)
+        else:
+            v.quantize_mx(T.ct[:], T.pt[:], T.t[:, HW:]).then_inc(sem.qt, 1)
     selectors()
 
-    dsts, land = {"lo": (["mid"], "a"), "mid": (["s"], "a"), "hi": (["s", "f"], "b")}[role]
-    g.wait_ge(sem.qt, 1)
-    send([home[d] for d in dsts], True, "qt", land)
-    send([home[d] for d in dsts], False, "pt", land)
+    moves = {"lo": [(home["mid"], "x", even)],
+             "mid": [(home["s"], "x", even)],
+             "hi": [(home["s"], "y", even), (home["f"], "y", odd)]}[role]
+    for part, src, ready in (("1", "q", "q1"), ("2", "t", "qt")):
+        g.wait_ge(sem[ready], 1)
+        for kind in "cp":
+            send(kind, part, src, H, *moves)
 
-    pe.wait_ge(sem.qt, 1)
     pe.wait_ge(sem.qs, W)
-    yk = 1
-    add(1, "qt", "pt", True, False)
-    order = ("b", "a")
+    pe.wait_ge(sem.qt, 1)
     if role == "mid":
-        wait_in(pe, "a")
-        add(1, "xa", "za", False, True, "u")
-        requantise(1, "u", "t2", "qu", "pu", "qu")
+        add(1, "t", True, False)
+        wait_in(pe, "x", *halves)
+        add(1, "x", False, True, "u")
+        requantise(1)
         g.wait_ge(sem.qu, 1)
-        send([far["lo"], home["hi"]], True, "qu", "a")
-        send([far["lo"], home["hi"]], False, "pu", "a")
-        yk = 0
-        add(0, "qt", "pt", True, False)
-        order = ("a", "b")
+        for kind in "cp":
+            send(kind, "w", "u", 0, (far["lo"], "x", out), (home["hi"], "x", stay))
 
-    for n, x in enumerate(order):
-        wait_in(pe, x)
-        add(yk, "x" + x, "z" + x, False, n == 1, "y" if n == 1 else None)
+    add(0, "t", True, False)
+    if role == "mid":
+        add(0, "x", False, False)
+        wait_in(pe, "y", "cw", "pw")
+        add(0, "y", False, True, "y")
+    else:
+        wait_in(pe, "y", "c1", "c2", "pw")
+        add(0, "y", False, False)
+        wait_in(pe, "x", "cw", "pw")
+        add(0, "x", False, True, "y")
     for i in range(W):
-        a = i in alt
-        (act if a else v).wait_ge(sem["y%d" % i], 1)
-        o = (TW // 2) * (i // 2)
-        copy(a, T.yo[:, o + i % 2:o + TW // 2:2], bank(yk, i)).then_inc(sem["e%d" % i], 1)
+        h, b = i // 2, i % 2
+        (v if b else act).wait_ge(sem["y%d" % i], 1)
+        for k in range(2):
+            copy(b == 0, T.yo[:, HW * h + 2 * k + b:HW * h + HW:W], bank(0, i, H * k, H)).then_inc(sem["e%d" % i], 1)
     for h in range(2):
-        g.sync.wait_ge(sem["e%d" % (2 * h)], 1)
-        g.sync.wait_ge(sem["e%d" % (2 * h + 1)], 1)
-        cols = slice(TW // 2 * h, TW // 2 * h + TW // 2)
+        g.sync.wait_ge(sem["e%d" % (2 * h)], 2)
+        g.sync.wait_ge(sem["e%d" % (2 * h + 1)], 2)
+        cols = slice(HW * h, HW * h + HW)
         g.sync.dma_start(T.y[:, cols], T.yo[:, cols]).then_inc(sem.stored, 16)
     g.sync.wait_ge(sem.stored, 32)
     g.wait_ge(sem.sent, sent[0])

from concourse.bass import DstId, RemoteDMATransfer
from concourse.mybir import dt, AluOpType, ActivationFunctionType

SIM = 16
W = 4
NCOL = 128
H = NCOL // 2
TW = W * NCOL
HW = TW // 2
BANK = 512
CODES = "float8_e4m3fn_x4"
WIDE = 8

SCRATCH = {
    "ta": ("sbuf", [128, W * TW], "bfloat16"),
    "tb": ("sbuf", [128, TW], "bfloat16"),
    "sel": ("sbuf", [128, TW + W], "bfloat16"),
    "t": ("sbuf", [128, 3 * HW], "bfloat16"),
    "tu": ("sbuf", [128, TW], "bfloat16"),
    "yo": ("sbuf", [128, TW], "float32"),
    "acc": ("psum", [128, 2 * W * BANK], "float32"),
}
for _k, _n in {"s": TW,
               "a": TW, "b": NCOL,
               "q": NCOL,
               "t": NCOL,
               "u": NCOL,
               "x": NCOL,
               "y": NCOL,
               }.items():
    SCRATCH["c" + _k] = ("sbuf", [128, _n], CODES)
    SCRATCH["p" + _k] = ("sbuf", [128, _n], "uint8")

SEMAPHORES = (["ld_b", "ld_0", "ld_1", "ones", "sel", "zero", "qs", "qb", "q1", "qt", "qu", "sent", "stored"]
              + ["%s%s%s" % (b, k, p) for b in "xy" for k in "cp" for p in "12w"]
              + ["%s%d" % (k, i) for k in ("qa", "m", "k", "u", "v", "y", "e") for i in range(W)])
PART = {"1": slice(0, H), "2": slice(H, NCOL), "w": slice(0, NCOL)}


def roles(T, topo):
    out = []
    n = len(T.cores) // 2
    for h in range(2):
        tri = T.cores[n * h:n * h + n]
        far = T.cores[n * (1 - h)]
        free = [c for c in range(SIM) if T.rank_of(c) is None and topo.chip(c) == topo.chip(tri[0])
                and topo.may_write(c, far)]
        out.append({"lo": tri[0], "mid": tri[1], "hi": tri[2],
                    "s": [c for c in free if topo.die(c) == topo.die(tri[2])][-1],
                    "f": [c for c in free if topo.die(c) != topo.die(tri[2])][0]})
    return out


def rank_program(g, core, T, topo):
    both = roles(T, topo)
    home = [r for r in both if topo.chip(r["lo"]) == topo.chip(core)][0]
    far = [r for r in both if r is not home][0]
    role = ([k for k in home if home[k] == core] or [None])[0]
    if role is None:
        return
    sem = T.sem
    sent = [0]

    def engines(m):
        return [e for e in range(m.bit_length()) if (m >> e) & 1]

    def send(kind, part, src, at, *moves):
        n = PART[part].stop - PART[part].start
        tr = []
        for dst, buf, eng in moves:
            rid, pid, _ = topo.addr(dst)
            o, i = T[kind + buf][:, PART[part]], T[kind + src][:, at:at + n]
            if kind == "c":
                o, i = o.bitcast(dt.uint8), i.bitcast(dt.uint8)
            tr.append((o, i, sem[buf + kind + part], pid, rid, sum(1 << e for e in eng)))
            sent[0] += len(eng)
        if len(tr) == 1:
            o, i, s, pid, rid, m = tr[0]
            g.remote_dma(o, i, s, sem.sent, pid, rid, m)
        else:
            g.remote_dma_fused([RemoteDMATransfer(dst_ids=[DstId(rid=rid, pnc=pid)], dma_engine_mask=m, remote_sem=s,
                                                  src=i, dst=o) for o, i, s, pid, rid, m in tr], local_sem=sem.sent)

    def wait_in(q, buf, *arrivals):
        for a in arrivals:
            q.wait_ge(sem[buf + a], WIDE)

    here = engines(topo.mask(core, home["lo" if role != "lo" else "hi"]))
    even, odd = here[0::2], here[1::2]
    if role in ("mid", "s", "f"):
        out = engines(topo.mask(core, far["lo"]))
        stay = [e for e in here if e not in out]

    def relay(dst):
        for part, at in (("1", 0), ("2", H)):
            wait_in(g, "y", "c" + part)
            send("c", part, "y", at, (dst, "y", out))
        wait_in(g, "y", "p1", "p2")
        send("p", "w", "y", 0, (dst, "y", out))

    if role == "f":
        relay(far["lo"])
        g.wait_ge(sem.sent, sent[0])
        return

    v, pe, act = g.vector, g.tensor, g.scalar

    def w(i):
        return slice(NCOL * i, NCOL * i + NCOL)

    def bank(k, i, lo=0, n=NCOL):
        o = BANK * (W * k + i) + lo
        return T.acc[:, o:o + n]

    if role != "s":
        act.dma_start(T.tb[:], T.b[:]).then_inc(sem.ld_b, 16)
        for k in range(2):
            cols = slice(2 * TW * k, 2 * TW * k + 2 * TW)
            g.sync.dma_start(T.ta[:, cols], T.a[:, cols]).then_inc(sem["ld_%d" % k], 16)

    v.memset(T.sel[:], 1.0).then_inc(sem.ones, 1)
    g.wait_ge(sem.ones, 1)
    g.affine_select(T.sel[:], T.sel[:], [[-1, TW + W]], AluOpType.is_equal, 0.0, W - 1, W).then_inc(sem.sel, 1)

    def selectors():
        v.wait_ge(sem.sel, 1)
        for i in range(W):
            v.quantize_mx(T.cs[:, w(i)], T.ps[:, w(i)], T.sel[:, W - 1 - i:W - 1 - i + TW]).then_inc(sem.qs, 1)

    def add(k, buf, first, last, done=None):
        for i in range(W):
            c = pe.matmul_mx(bank(k, i), T.cs[:, w(i)], T.ps[:, w(i)], T["c" + buf][:, :NCOL], T["p" + buf][:, :NCOL], first, last)
            if done:
                c.then_inc(sem["%s%d" % (done, i)], 1)

    def copy(on_act, out_, in_):
        if on_act:
            return act.activation(out_, in_, ActivationFunctionType.Copy)
        return v.tensor_copy(out_, in_)

    def requantise(k):
        for i in range(W):
            a = i % 2 == 0
            (act if a else v).wait_ge(sem["u%d" % i], 1)
            copy(a, T.tu[:, i:TW:W], bank(k, i)).then_inc(sem["v%d" % i], 1)
        for i in range(W):
            v.wait_ge(sem["v%d" % i], 1)
        v.quantize_mx(T.cu[:], T.pu[:], T.tu[:]).then_inc(sem.qu, 1)

    halves = ("c1", "p1", "c2", "p2")

    if role == "s":
        selectors()
        pe.wait_ge(sem.qs, W)
        wait_in(pe, "x", *halves)
        add(0, "x", True, False)
        wait_in(pe, "y", *halves)
        add(0, "y", False, True, "u")
        requantise(0)
        relay(far["hi"])
        g.wait_ge(sem.qu, 1)
        for kind in "cp":
            send(kind, "w", "u", 0, (far["mid"], "y", out))
        g.wait_ge(sem.sent, sent[0])
        return

    v.memset(T.t[:, :HW], 0.0).then_inc(sem.zero, 1)
    v.wait_ge(sem.ld_b, 16)
    v.quantize_mx(T.cb[:], T.pb[:], T.tb[:]).then_inc(sem.qb, 1)
    pe.wait_ge(sem.qb, 1)
    for k in range(2):
        v.wait_ge(sem["ld_%d" % k], 16)
        for i in (2 * k, 2 * k + 1):
            v.quantize_mx(T.ca[:, w(i)], T.pa[:, w(i)], T.ta[:, TW * i:TW * i + TW]).then_inc(sem["qa%d" % i], 1)
            pe.wait_ge(sem["qa%d" % i], 1)
            pe.matmul_mx(bank(0, i), T.ca[:, w(i)], T.pa[:, w(i)], T.cb[:], T.pb[:], True, True).then_inc(sem["m%d" % i], 1)
        for b in range(2):
            i = 2 * k + b
            (v if b else act).wait_ge(sem["m%d" % i], 1)
            for h in range(2):
                o = HW * (1 + k)
                copy(b == 0, T.t[:, o + 2 * h + b:o + HW:W], bank(0, i, H * h, H)).then_inc(sem["k%d" % i], 1)
        v.wait_ge(sem["k%d" % (2 * k)], 2)
        v.wait_ge(sem["k%d" % (2 * k + 1)], 2)
        if k == 0:
            v.wait_ge(sem.zero, 1)
            v.quantize_mx(T.cq[:], T.pq[:], T.t[:, :TW]).then_inc(sem.q1, 1)
        else:
            v.quantize_mx(T.ct[:], T.pt[:], T.t[:, HW:]).then_inc(sem.qt, 1)
    selectors()

    moves = {"lo": [(home["mid"], "x", even)],
             "mid": [(home["s"], "x", even)],
             "hi": [(home["s"], "y", even), (home["f"], "y", odd)]}[role]
    for part, src, ready in (("1", "q", "q1"), ("2", "t", "qt")):
        g.wait_ge(sem[ready], 1)
        for kind in "cp":
            send(kind, part, src, H, *moves)

    pe.wait_ge(sem.qs, W)
    pe.wait_ge(sem.qt, 1)
    if role == "mid":
        add(1, "t", True, False)
        wait_in(pe, "x", *halves)
        add(1, "x", False, True, "u")
        requantise(1)
        g.wait_ge(sem.qu, 1)
        for kind in "cp":
            send(kind, "w", "u", 0, (far["lo"], "x", out), (home["hi"], "x", stay))

    add(0, "t", True, False)
    if role == "mid":
        add(0, "x", False, False)
        wait_in(pe, "y", "cw", "pw")
        add(0, "y", False, True, "y")
    else:
        wait_in(pe, "y", "c1", "c2", "pw")
        add(0, "y", False, False)
        wait_in(pe, "x", "cw", "pw")
        add(0, "x", False, True, "y")
    for i in range(W):
        h, b = i // 2, i % 2
        (v if b else act).wait_ge(sem["y%d" % i], 1)
        for k in range(2):
            copy(b == 0, T.yo[:, HW * h + 2 * k + b:HW * h + HW:W], bank(0, i, H * k, H)).then_inc(sem["e%d" % i], 1)
    for h in range(2):
        g.sync.wait_ge(sem["e%d" % (2 * h)], 2)
        g.sync.wait_ge(sem["e%d" % (2 * h + 1)], 2)
        cols = slice(HW * h, HW * h + HW)
        g.sync.dma_start(T.y[:, cols], T.yo[:, cols]).then_inc(sem.stored, 16)
    g.sync.wait_ge(sem.stored, 32)
    g.wait_ge(sem.sent, sent[0])
